import numpy as np, ml_dtypes
CORES = [16,17,18,19,32,33,34,35]
N = 8
import mx_ref
BF = ml_dtypes.bfloat16
def gentries(a):
    return np.ascontiguousarray(a.reshape(8, 16, -1).transpose(0, 2, 1)).reshape(8, -1)
def gtable(e):
    e = np.asarray(e); return np.ascontiguousarray(e.reshape(8, -1, 16).transpose(0, 2, 1)).reshape(128, -1).astype(np.int32)
def gcols(t, e):
    v = np.concatenate([t.reshape(8, 16, -1, 4), np.zeros((8, 16, 1, 4), BF)], axis=2)
    return np.ascontiguousarray(np.stack([v[g][:, e[g]] for g in range(8)])).reshape(128, -1)
def tile(rs):
    return np.stack(rs, axis=2).reshape(128, -1).astype(BF)
def cut(t, i, w=512):
    return t[:, w * i:w * i + w]
def pick(q, e):
    c = np.concatenate([q[0].reshape(128, -1, 4), np.zeros((128, 1, 4), np.uint8)], axis=1); s = np.concatenate([q[1], np.ones((16, 1), np.uint8)], axis=1)
    return (np.ascontiguousarray(c[:, e].reshape(128, -1)), np.ascontiguousarray(s[:, e]))
def join(*qs):
    return (np.concatenate([q[0] for q in qs], axis=1), np.concatenate([q[1] for q in qs], axis=1))
def put(q, e, v):
    c, s = q[0].reshape(128, -1, 4).copy(), q[1].copy(); c[:, e] = v[0].reshape(128, -1, 4); s[:, e] = v[1]
    return (c.reshape(128, -1), s)
def pk(c, s):
    return (np.ascontiguousarray(c), mx_ref.live(s))
def emit(q):
    return q[0], q[1]
def packed(v, rng):
    q = [mx_ref.quantize(np.ascontiguousarray(v[r])) for r in range(N)]
    return np.stack([a for a, b in q]), np.stack([mx_ref.plane(b, rng) for a, b in q])
def values_of_codes():
    e, c = np.zeros((128, 128, 4), np.float32), np.zeros((128, 2, 4), np.uint8)
    e[np.arange(128), np.arange(128), 0] = 1
    c[:127, :, 0] = np.arange(256).reshape(2, 128).T[:127]
    return mx_ref.matmul(mx_ref.quantize(e.reshape(128, 512).astype(BF)), (c.reshape(128, 8), np.full((16, 2), 127, np.uint8))).T.reshape(-1).astype(np.float64)
CODE_VALUE, SCALE_VALUE = values_of_codes(), 2.0 ** (np.arange(256) - 127.0)
def decode(q):
    return (CODE_VALUE[q[0]].reshape(16, 8, -1, 4) * SCALE_VALUE[q[1]][:, None, :, None] + 0.0).reshape(128, -1).astype(np.float32)
def f(rng, *shape):
    return mx_ref.flush((rng.standard_normal(shape, dtype=np.float32) * np.exp2(rng.integers(-2, 3, shape[:-1] + (1,)))).astype(BF))
def wide(rng, *shape, cols=0):
    v = rng.standard_normal(shape, dtype=np.float32) * np.exp2(rng.integers(-12, 13, shape)).astype(np.float32)
    if cols: v *= np.repeat(np.exp2(rng.integers(-cols, cols + 1, shape[:-2] + (1, shape[-1] // 4))) * (rng.random(shape[:-2] + (1, shape[-1] // 4)) > 0.0625), 4, axis=-1).astype(np.float32)
    return mx_ref.flush(v.astype(BF))
C, B, R = 384, 24, 3
STEP = [1, 2, 4]
def slides(s):
    n = 8 * B
    i = np.arange(n)
    who = np.full((n, 5, 5), -9)
    key = np.full((n, 5, 5), -np.inf, np.float32)
    who[:, :4, :4] = np.arange(16).reshape(4, 4)
    key[:, :4, :4] = s.reshape(n, 4, 4)
    left = np.zeros((4, n), np.int64)
    for k in range(4):
        left[k] = who[:, 0, 0]
        y, c = np.zeros(n, np.int64), np.zeros(n, np.int64)
        for m in range(6):
            right = key[i, y, c + 1] >= key[i, y + 1, c]
            y2, c2 = np.where(right, y, y + 1), np.where(right, c + 1, c)
            go = who[i, y2, c2] >= 0
            j = i[go]
            who[j, y[go], c[go]] = who[j, y2[go], c2[go]]
            key[j, y[go], c[go]] = key[j, y2[go], c2[go]]
            y, c = np.where(go, y2, y), np.where(go, c2, c)
        who[i, y, c] = -1 - k
        key[i, y, c] = -np.inf
    b = np.arange(B)
    w = who[:, :4, :4].reshape(8, B, 16)
    stand = np.where(w >= 0, 16 * b[:, None] + w, C + B * (-1 - w) + b[:, None]).reshape(8, C)
    return (left.reshape(4, 8, B) + 16 * b).transpose(1, 0, 2).reshape(8, 4 * B), stand
def big(v):
    v = v.astype(np.float32)
    v[np.abs(v) < np.float32(2.0 ** -16)] = 0
    return v.astype(BF)
def seats(rng):
    return np.argsort(rng.random((N, 8, C)), axis=2)
def seated(e, a):
    s = np.zeros_like(a)
    np.put_along_axis(s, e, a, axis=2)
    return s
def digits(s):
    return ((s[..., None] >> np.arange(4)) & 1) * np.exp2(np.arange(4.0))
def numbers_of(rng, e):
    return {"x": big(f(rng, N, 128, 4 * C)), "p": np.stack([gtable(e[r]) for r in range(N)]), "u": np.array(f(rng, N, 128, 512)), "v": np.array(f(rng, N, 128, 512))}
def layers(rng, still=()):
    w = big(f(rng, N, 128, 2048)).reshape(N, 8, 16, 4, 8, 16, 4)
    for i in still:
        w[:, :, i] = 0
        w[:, :, :, :, :, i] = 0
    return w.reshape(N, 128, 2048)
def weights(rng, w):
    c, s = packed(np.ascontiguousarray(w).reshape(N, 128, 2048), rng)
    return {"wc": c, "ws": s}
def signs(rng):
    return np.stack([rng.permutation(8) % 2 * 2.0 - 1.0 for r in range(N)])
def setup_inputs(rng):
    return {**numbers_of(rng, seats(rng)), **weights(rng, layers(rng))}
def setup_inputs_ties(rng):
    d = numbers_of(rng, seats(rng))
    e = rng.permutation(N)
    x = d["x"].reshape(N, 8, 16, C, 4)
    for r in range(N):
        k = np.zeros(C, int) if r == e[0] else rng.permutation(C) % 3
        a = x[r][:, :8, :3].copy()
        a[:, :, 2] = 0
        x[r][:, :8] = a[:, :, k]
    x[e[1]] = 0
    u = d["u"].reshape(N, 8, 16, 8, 16, 4)
    k = u.copy()
    u[:, :, :, :, 0] = 0
    for g in range(8): u[:, g, :8, g, 0] = k[:, g, :8, g, 0]
    return {"x": x.reshape(N, 128, 4 * C), "p": d["p"], "u": u.reshape(N, 128, 512), "v": d["v"], **weights(rng, layers(rng, range(8)))}
def setup_inputs_near(rng):
    e = seats(rng)
    d = numbers_of(rng, e)
    x = d["x"].astype(np.float32).reshape(N, 8, 16, C, 4)
    u = d["u"].reshape(N, 128, 128, 4)
    u[:, :, ::16] = 0
    o, c = rng.permutation(N) % 4, signs(rng)
    s = seated(e, np.argsort(rng.random((N, 8, B, 16)), axis=3).reshape(N, 8, C))
    x[:, :, 0] = 0
    x[:, :, 9] = 0
    for r in range(N):
        size = 2.0 ** -23 if o[r] < 2 else 2.0 ** -30
        if o[r] < 2:
            x[r, :, 0, :, 0] = c[r][:, None]
            x[r, :, 9, :, 0] = c[r][:, None] * 2.0 ** -12
            for i in rng.permutation(8)[:4]: x[r, i, 0, rng.integers(C), 0] *= np.float32(2.0 ** 30)
        x[r, :, 8] = digits(s[r]) * (-size if o[r] == 3 else size) + 0.0
        x[r, :, 10:] = rng.integers(4, 8, (8, 6, C, 4)) * rng.choice([-1.0, 1.0], (8, 6, C, 4)) * size
        k = 1.0 if o[r] == 0 else 2.0 ** -30
        for h in range(0, 128, 16):
            u[r, h, h, 0] = k
            u[r, h + 8, h] = k
            u[r, h + 9, h, 0] = k
    return {"x": x.reshape(N, 128, 4 * C).astype(BF), "p": d["p"], "u": u.reshape(N, 128, 512), "v": d["v"], **weights(rng, layers(rng, [0, 8, 9, 10, 11, 12, 13, 14, 15]))}
def setup_inputs_huge(rng):
    d = numbers_of(rng, seats(rng))
    c = np.stack([rng.permutation(C) % 2 * 2.0 - 1.0 for r in range(N)])
    c[rng.permutation(N) < N // 2] = -1
    x = 2.0 ** 30 * (1 - 0.0625 * (rng.random((N, 128, C, 4)) < 0.25)) * c[:, None, :, None]
    u = d["u"].reshape(N, 128, 128, 4)
    a = 2.0 ** 30 * (1 - 0.0625 * (rng.random((N, 128, 8, 4)) < 0.25)) * signs(rng)[:, None, :, None]
    u[:, :, ::16] = a.astype(np.float32).astype(BF)
    w = np.zeros((N, 128, 4, 128, 4), np.float32)
    i = np.arange(128)
    for b in range(4): w[:, i, b, i, b] = -32
    return {"x": x.astype(np.float32).reshape(N, 128, 4 * C).astype(BF), "p": d["p"], "u": u.reshape(N, 128, 512), "v": d["v"], **weights(rng, w.astype(BF))}
def setup_inputs_moves(rng):
    e = seats(rng)
    i = rng.permutation(N)
    e[i[2]] = np.arange(C)
    d = numbers_of(rng, e)
    a = np.arange(16)
    s = np.argsort(rng.random((N, 8, B, 16)), axis=3)
    k = np.argsort(rng.random((N, 8, B)), axis=2) % 4
    k[i[0]], k[i[1]] = 0, 1
    s[k == 0] = a % 4 * 4 + a // 4
    s[k == 1] = a
    x = d["x"].reshape(N, 8, 16, C, 4)
    x[:, :, 8] = digits(seated(e, s.reshape(N, 8, C))).astype(np.float32).astype(BF)
    u = d["u"].reshape(N, 128, 128, 4)
    u[:, :, ::16] = 0
    for h in range(0, 128, 16): u[:, h + 8, h] = 1
    return {"x": x.reshape(N, 128, 4 * C), "p": d["p"], "u": u.reshape(N, 128, 512), "v": d["v"], **weights(rng, layers(rng, range(8, 16)))}
def setup_inputs_spread(rng):
    d = setup_inputs(rng)
    d["x"] = big(wide(rng, N, 128, 4 * C, cols=6))
    return d
def check_inputs(d):
    b = []
    for k in ("x", "u", "v"):
        a = np.abs(d[k].astype(np.float32))
        if not (np.isfinite(a).all() and ((a == 0) | (a >= 2.0 ** -30) & (a <= 2.0 ** 30)).all()): b.append("a value of " + k)
    none, least, most = [emit(mx_ref.quantize(np.full((128, 16), k, np.float32).astype(BF)))[1][0, 0] for k in (0.0, 2.0 ** -30, 2.0 ** 30)]
    for r in range(N):
        if not (np.sort(gentries(d["p"][r]), axis=1) == np.arange(C)).all(): b.append("p: a group's entries aren't all columns, each once")
        if ((d["wc"][r] == 0x7F) | (d["wc"][r] == 0xFF)).any(): b.append("wc: a code that is no number")
        s = mx_ref.live(d["ws"][r])
        if ((s != none) & ((s < least) | (s > most))).any(): b.append("ws: a scale out of range")
    return b
def reference(x, p, u, v, wc, ws):
    qu = [mx_ref.quantize(u[r]) for r in range(N)]
    lay = [pk(wc[r], ws[r]) for r in range(N)]
    seat = [gentries(p[r]) for r in range(N)]
    slots = np.tile(C + np.arange(4 * B), (8, 1))
    now = [x[r] for r in range(N)]
    for t in range(R):
        sent, fill = [], []
        for r in range(N):
            s = mx_ref.matmul(qu[r], mx_ref.quantize(now[r]))
            left, stand = slides(np.take_along_axis(s[::16], seat[r], axis=1))
            sent.append(mx_ref.quantize(gcols(now[r], np.take_along_axis(seat[r], left, axis=1))))
            fill.append(np.take_along_axis(np.concatenate([seat[r], slots], axis=1), stand, axis=1))
        came = decode(join(*sent)).astype(BF)
        made = []
        for r in range(N):
            z = gcols(np.concatenate([now[r], cut(came, (r - STEP[t]) % N, 16 * B)], axis=1), fill[r])
            q = mx_ref.quantize(z)
            made.append(tile([np.maximum(mx_ref.matmul(pick(lay[r], np.arange(128 * b, 128 * b + 128)), q), np.float32(0.0)) * np.float32(0.015625) + z[:, b::4].astype(np.float32) for b in range(4)]))
        now = made
    y, ol = np.zeros((N, 128, C), np.float32), np.zeros((N, 8, C), np.float32)
    oc, osc = np.zeros((N, 128, 4 * C), np.uint8), np.zeros((N, 16, C), np.uint8)
    for r in range(N):
        q = mx_ref.quantize(now[r])
        y[r] = mx_ref.matmul(mx_ref.quantize(v[r]), q)
        ol[r] = fill[r]
        oc[r], osc[r] = emit(q)
    return {"y": y, "ol": ol, "oc": oc, "osc": osc}

import numpy as np
from concourse.mybir import dt, AluOpType, ActivationFunctionType

ALU = AluOpType
ACT = ActivationFunctionType
C, NB, ROUNDS = 384, 24, 3
STEP = [1, 2, 4]
BIG = 1.0e29
CH = [(0, 128), (128, 256), (256, 384)]
F32, BF, I32, U16, X4, U8 = "float32", "bfloat16", "int32", "uint16", "float8_e4m3fn_x4", "uint8"

PIECES = [[(0, 192, False), (192, 384, False)],
          [(0, 128, False), (128, 256, False), (256, 384, False)],
          [(0, 128, True), (128, 256, True), (256, 384, False)]]
PICKED = [False, False, False]
QUANT_F_AFTER = "A3"

SLIDES = ("R0 a0 b0 M0 c0 o0 n0 t0 u0 W0 K1 A1 R1 C1 a1 b1 M1 c1 B1 o1 n1 W1 t1 u1 A2 K2 C2 B2 R2 M2 e a2 g b2 l c2 s "
          "o2 n2 t2 u2 W2 K3 A3 R3 C3 a3 B3 b3 c3 o3 X3 W3").split()
LAYER = ("C2v C1v F0v C0v F1a C3v F2a G02a G01v G00a G03v G22v G10a G12a QV0v G13v G23v G11a QV1v R00a R02a A00v R03a "
         "A02v A03v R01a A01v G20a G21a QV2v R10a R11a QT0v A10v R12a R13a A11v A12v R21a A13v R22a R23a QT1v A21v A22v "
         "R20a A23v A20v T0a QT2v T1a T2v").split()

SCRATCH = {
    "pI": ("sbuf", [128, 24], I32), "pid": ("sbuf", [128, 4], I32), "ti": ("sbuf", [128, 4], I32),
    "dif": ("sbuf", [128, 128], F32), "tc": ("sbuf", [128, 32], F32), "i2": ("sbuf", [128, 2], F32),
    "i4": ("sbuf", [128, 4], F32), "cf": ("sbuf", [128, 8], F32), "lam": ("sbuf", [128, 4], F32),
    "lgo": ("sbuf", [128, 2], U16), "zer": ("sbuf", [128, 10, 5], F32),
    "dup": ("sbuf", [128, 64], F32), "dtr": ("sbuf", [128, 64], F32), "kof": ("sbuf", [128, 32], F32),
    "koff": ("sbuf", [128, 32], U16), "p4": ("sbuf", [128, 32], F32), "w0": ("sbuf", [128, 32], F32),
    "Ef": ("sbuf", [128, 2048], BF), "Eq": ("sbuf", [128, 512], X4), "Es": ("sbuf", [128, 512], U8),
    "ub": ("sbuf", [128, 512], BF), "uq": ("sbuf", [128, 128], X4), "us": ("sbuf", [128, 128], U8),
    "vb": ("sbuf", [128, 512], BF), "vq": ("sbuf", [128, 128], X4), "vs": ("sbuf", [128, 128], U8),
    "wq": ("sbuf", [128, 512], X4), "wsc": ("sbuf", [128, 512], U8),
    "ks": ("sbuf", [128, 384], F32), "kg": ("sbuf", [128, 512], F32), "kt": ("sbuf", [128, 512], F32),
    "L": ("sbuf", [128, 10, 5], F32), "M": ("sbuf", [128, 36], F32), "non": ("sbuf", [128, 36], F32),
    "t1": ("sbuf", [128, 36], F32), "t2": ("sbuf", [128, 36], F32),
    "WO": ("sbuf", [128, 392], F32), "D3": ("sbuf", [128, 108], F32), "WF": ("sbuf", [128, 96], F32),
    "lg": ("sbuf", [128, 32], F32), "lt": ("sbuf", [128, 32], F32), "wt": ("sbuf", [128, 32], F32),
    "voff": ("sbuf", [128, 96], U16),
    "o1": ("sbuf", [128, 32], F32), "o2": ("sbuf", [128, 32], F32), "o3": ("sbuf", [128, 32], F32),
    "o4": ("sbuf", [128, 32], F32), "olb": ("sbuf", [128, 32], F32),
    "V": ("sbuf", [128, 1536], BF), "qv": ("sbuf", [128, 384], X4), "sv": ("sbuf", [128, 384], U8),
    "rl": ("sbuf", [128, 1536], F32), "Dt": ("sbuf", [128, 1536], BF), "yb": ("sbuf", [128, 384], F32),
    "rq": ("sbuf", [128, 384], X4), "rs": ("sbuf", [128, 384], U8),
    "Ft": ("sbuf", [128, 512], BF), "zb": ("sbuf", [128, 512], BF),
    "ps": ("psum", [128, 4096], F32),
}
for _k in range(4):
    SCRATCH["K%d" % _k] = ("sbuf", [128, 10, 5], F32)
    SCRATCH["Y%d" % _k] = ("sbuf", [128, 10, 5], F32)
    SCRATCH["Z%d" % _k] = ("sbuf", [128, 108], F32)
    SCRATCH["TW%d" % _k] = ("sbuf", [128, 1920], BF)
    SCRATCH["qt%d" % _k] = ("sbuf", [128, 384], X4)
    SCRATCH["st%d" % _k] = ("sbuf", [128, 384], U8)
for _k in range(ROUNDS):
    SCRATCH["lq%d" % _k] = ("sbuf", [128, 384], X4)
    SCRATCH["ls%d" % _k] = ("sbuf", [128, 384], U8)
    SCRATCH["fq%d" % _k] = ("sbuf", [128, 128], X4)
    SCRATCH["fs%d" % _k] = ("sbuf", [128, 128], U8)
    SCRATCH["sl%d" % _k] = ("sbuf", [128, 24], U16)
    SCRATCH["ll%d" % _k] = ("sbuf", [128, 24], U16)

SEMAPHORES = ["cv", "ca", "cp", "cg", "loc", "sto", "dp", "dx0", "dx1", "du", "dv", "dw", "dz"]
for _k in range(ROUNDS):
    SEMAPHORES += ["a0_%d" % _k, "a1_%d" % _k, "a2_%d" % _k, "al_%d" % _k, "r0_%d" % _k, "r1_%d" % _k, "r2_%d" % _k]


def picked(t, src, dst, topo):
    return PICKED[t] and topo.chip(src) != topo.chip(dst)


def relay_of(t, src, dst, T, topo):
    n = len(T.cores)
    crossing = [r for r in range(n) if topo.chip(T.cores[r]) == topo.chip(src)
                and topo.chip(T.cores[(r + STEP[t]) % n]) != topo.chip(src)]
    if topo.chip(src) == topo.chip(dst):
        return None
    far = []
    for c in range(64):
        if topo.mates(topo.chip(c), topo.chip(dst)) and topo.die(c) == topo.die(src) and topo.may_write(c, dst):
            far.append(c)
    senders = [T.cores[r] for r in crossing]
    able = [s for s in senders if far and topo.may_write(s, far[0])]
    if src in able:
        return far[able.index(src) % len(far)]
    other = [c for c in topo.cores_of(src) if topo.die(c) != topo.die(src) and T.rank_of(c) is None]
    rest = [s for s in senders if s not in able]
    return other[rest.index(src) % len(other)]


def write(g, T, topo, src, dst, out_ap, in_ap, sem):
    rid, pid, _ = topo.addr(dst)
    g.remote_dma(out_ap, in_ap, T.sem[sem], T.sem.loc, pid, rid, topo.mask(src, dst))
    return len(topo.engines(src, dst))


def relay_program(g, core, T, topo):
    n = len(T.cores)
    sent = 0
    for t in range(ROUNDS):
        for r in range(n):
            src, dst = T.cores[r], T.cores[(r + STEP[t]) % n]
            if relay_of(t, src, dst, T, topo) != core:
                continue
            for j, (a, b, far) in enumerate(PIECES[t]):
                if not far or picked(t, src, dst, topo):
                    continue
                g.wait_ge(T.sem["r%d_%d" % (j, t)], 2 * len(topo.engines(src, core)))
                sem = "a%d_%d" % (j, t)
                sent += write(g, T, topo, core, dst, T["lq%d" % t][:, a:b].bitcast(dt.uint8), T.rq[:, a:b].bitcast(dt.uint8), sem)
                sent += write(g, T, topo, core, dst, T["ls%d" % t][:, a:b], T.rs[:, a:b], sem)
    if sent:
        g.wait_ge(T.sem.loc, sent)


def rank_program(g, core, T, topo):
    rank = T.rank_of(core)
    if rank is None:
        relay_program(g, core, T, topo)
        return
    n = len(T.cores)
    to = [T.cores[(rank + s) % n] for s in STEP]
    frm = [T.cores[(rank - s) % n] for s in STEP]
    sends_f = [picked(t, core, to[t], topo) for t in range(ROUNDS)]
    gets_f = [picked(t, frm[t], core, topo) for t in range(ROUNDS)]
    S = slice
    A = S(None)
    eng = {"g": g, "v": g.vector, "a": g.scalar, "p": g.tensor, "s": g.sync}
    csem = {"g": "cg", "v": "cv", "a": "ca", "p": "cp"}
    total = {}
    known = {q: {} for q in eng}
    toks = []
    lastw, lastr, index = {}, {}, {}
    for name, (where, shape, dty) in SCRATCH.items():
        size = int(np.prod(shape[1:]))
        index[name] = np.arange(size).reshape(shape[1:])
        lastw[name] = np.full(size, -1)
        lastr[name] = {}

    def ap(r):
        return T[r[0]][(A,) + tuple(r[1:])]

    def cells(r):
        c = index[r[0]][tuple(r[1:])].reshape(-1)
        if r[0] == "ps":
            b = int(c[0]) // 512
            c = np.arange(512 * b, 512 * b + 512)
        return c

    def wait(q, deps):
        for d in sorted(deps, reverse=True):
            sem, val, clock = toks[d]
            if known[q].get(sem, 0) >= val:
                continue
            eng[q].wait_ge(T.sem[sem], val)
            known[q][sem] = val
            for k2, v2 in clock.items():
                if known[q].get(k2, 0) < v2:
                    known[q][k2] = v2

    def note(tok, q, reads, writes):
        for r in reads:
            d = lastr[r[0]]
            if q not in d:
                d[q] = np.full(lastw[r[0]].size, -1)
            d[q][cells(r)] = tok
        for r in writes:
            lastw[r[0]][cells(r)] = tok

    def needs(reads, writes):
        deps = set()
        for r in reads:
            deps.update(np.unique(lastw[r[0]][cells(r)]).tolist())
        for r in writes:
            c = cells(r)
            deps.update(np.unique(lastw[r[0]][c]).tolist())
            for arr in lastr[r[0]].values():
                deps.update(np.unique(arr[c]).tolist())
        deps.discard(-1)
        return deps

    def op(q, fn, reads, writes, sem=None, after=()):
        writes = list(writes) + [r for r in reads if r[0] == "ps"]
        wait(q, needs(reads, writes) | set(after))
        inc = 16 if sem else 1
        sem = sem or csem[q]
        fn().then_inc(T.sem[sem], inc)
        total[sem] = total.get(sem, 0) + inc
        toks.append((sem, total[sem], dict(known[q])))
        note(len(toks) - 1, q if inc == 1 else sem + str(len(toks)), reads, writes)
        return len(toks) - 1

    def arrival(sem, val, writes):
        total[sem] = val
        toks.append((sem, val, {}))
        note(len(toks) - 1, sem, [], writes)

    def send(dst, out_ap, in_ap, sem, reads):
        wait("g", needs(reads, []))
        total["loc"] = total.get("loc", 0) + write(g, T, topo, core, dst, out_ap, in_ap, sem)

    def tt(o, a, b, alu):
        return op("v", lambda: g.vector.tensor_tensor(ap(o), ap(a), ap(b), alu), [a, b], [o])

    def ts(o, a, s1, op0, s2=None, op1=None):
        rd = [a] + [s for s in (s1, s2) if isinstance(s, tuple)]
        x1 = ap(s1) if isinstance(s1, tuple) else s1
        x2 = ap(s2) if isinstance(s2, tuple) else s2
        if op1 is None:
            return op("v", lambda: g.vector.tensor_scalar(ap(o), ap(a), x1, None, op0), rd, [o])
        return op("v", lambda: g.vector.tensor_scalar(ap(o), ap(a), x1, x2, op0, op1), rd, [o])

    def cp(q, o, a):
        if q == "v":
            return op("v", lambda: g.vector.tensor_copy(ap(o), ap(a)), [a], [o])
        return op("a", lambda: g.scalar.activation(ap(o), ap(a), ACT.Copy), [a], [o])

    def shift(o, a, bias):
        rd = [a] + ([bias] if isinstance(bias, tuple) else [])
        x = ap(bias) if isinstance(bias, tuple) else bias
        return op("a", lambda: g.scalar.activation(ap(o), ap(a), ACT.Identity, x, 1.0), rd, [o])

    def gather(q, o, win, off):
        if q == "v":
            return op("v", lambda: g.vector.tensor_copy(ap(o), ap(win).indirect(ap(off))), [win, off], [o])
        return op("a", lambda: g.scalar.activation(ap(o), ap(win).indirect(ap(off)), ACT.Copy), [win, off], [o])

    def scan(o, d0, d1, op0, op1):
        return op("v", lambda: g.vector.tensor_tensor_scan(ap(o), ap(d0), ap(d1), 0.0, op0, op1), [d0, d1], [o])

    def tr(o, a):
        return op("v", lambda: g.vector.transpose(ap(o), ap(a)), [a], [o])

    def fill(o, val):
        return op("v", lambda: g.vector.memset(ap(o), val), [], [o])

    def iota(o, pattern, base, cm, small=True):
        if small:
            return op("g", lambda: g.iota(ap(o), pattern, base, cm, allow_small_or_imprecise_dtypes=True), [], [o])
        return op("g", lambda: g.iota(ap(o), pattern, base, cm), [], [o])

    def quant(qn, sn, a, b, tile):
        o, s, i = (qn, S(a, b)), (sn, S(a, b)), (tile, S(4 * a, 4 * b))
        return op("v", lambda: g.vector.quantize_mx(ap(o), ap(s), ap(i)), [i], [o, s])

    def mm(bk, wq, ws, w0, xq, xs, a, b):
        o = ("ps", S(512 * bk, 512 * bk + b - a))
        l, ls, r, rs = (wq, S(w0, w0 + 128)), (ws, S(w0, w0 + 128)), (xq, S(a, b)), (xs, S(a, b))
        return op("p", lambda: g.tensor.matmul_mx(ap(o), ap(l), ap(ls), ap(r), ap(rs), True, True), [l, ls, r, rs], [o])

    def bank(b, w):
        return ("ps", S(512 * b, 512 * b + w))

    cur, right, down = (S(0, 9), S(0, 4)), (S(0, 9), S(1, 5)), (S(1, 10), S(0, 4))

    op("s", lambda: g.sync.dma_start(T.pI[:], T.p[:]), [], [("pI", A)], "dp")
    op("a", lambda: g.scalar.dma_start(T.TW0[:, 0:768], T.x[:, 0:768]), [], [("TW0", S(0, 768))], "dx0")
    op("s", lambda: g.sync.dma_start(T.ub[:], T.u[:]), [], [("ub", A)], "du")
    op("a", lambda: g.scalar.dma_start(T.TW0[:, 768:1536], T.x[:, 768:1536]), [], [("TW0", S(768, 1536))], "dx1")
    op("s", lambda: g.sync.dma_start(T.wq[:].bitcast(dt.uint8), T.wc[:]), [], [("wq", A)], "dw")
    op("s", lambda: g.sync.dma_start(T.wsc[:], T.ws[:]), [], [("wsc", A)], "dz")

    iota(("pid", A), [[0, 4]], 0, 1, small=False)
    iota(("dif", A), [[-1, 128]], 0, 1)
    iota(("i4", A), [[-4, 4]], 4 * C + 12, 0)
    iota(("i2", A), [[60, 2]], 326, 0)
    iota(("tc", A), [[0, 8], [1, 4]], 0, 0)
    fill(("zer", A, A), 0.0)
    fill(("dup", A), 0.0)
    fill(("p4", A), 0.0)
    ts(("ti", S(0, 1)), ("pid", S(0, 1)), 4, ALU.arith_shift_right, 1, ALU.bitwise_and)
    ts(("ti", S(1, 2)), ("pid", S(0, 1)), 2, ALU.arith_shift_right, 3, ALU.bitwise_and)
    ts(("ti", S(2, 3)), ("pid", S(0, 1)), 31, ALU.bitwise_and)
    fill(("WO", S(50, 60, 3)), 1.0e6)
    ts(("cf", S(0, 1)), ("ti", S(0, 1)), -1.0, ALU.mult, 1.0, ALU.add)
    ts(("cf", S(1, 2)), ("ti", S(0, 1)), 1.0, ALU.mult)
    ts(("cf", S(2, 3)), ("ti", S(1, 2)), 108.0, ALU.mult)
    ts(("cf", S(3, 4)), ("ti", S(2, 3)), 16.0, ALU.mult)
    ts(("cf", S(4, 5)), ("ti", S(2, 3)), 97.0, ALU.mult, float(25 * C + 72), ALU.add)
    ts(("lam", A), ("i4", A), ("cf", S(3, 4)), ALU.add)
    ts(("lgo", A), ("i2", A), ("cf", S(2, 3)), ALU.subtract)
    fill(("Ef", A), 0.0)
    for b in range(4):
        ts(("Ef", S(513 * b, 512 * b + 512, 4)), ("dif", A), 0.0, ALU.is_equal)
    zer = ("zer", A, A)
    cp("a", ("kt", S(0, 32)), ("zer", S(0, 8), S(0, 4)))
    cp("a", ("L", A, A), zer)
    for k in range(4):
        shift(("K%d" % k, A, A), zer, -BIG)
        cp("a", ("Z%d" % k, S(0, 108, 3)), ("zer",) + cur)
    shift(("L", S(1, 5), 0), ("zer", S(1, 5), 0), 1.0)
    shift(("L", S(6, 10), 0), ("zer", S(1, 5), 0), 1.0)
    shift(("Z2", S(2, 108, 3)), ("zer",) + cur, 1.0)
    for k in range(4):
        shift(("Y%d" % k, A, A), zer, ("lam", S(k, k + 1)))
    if any(sends_f):
        fill(("Ft", S(384, 512)), 0.0)
    if any(gets_f):
        fill(("zb", A), 0.0)
    for t in range(ROUNDS):
        if gets_f[t]:
            o, sc = ("lq%d" % t, S(96, 224)), ("ls%d" % t, S(96, 224))
            op("v", lambda: g.vector.quantize_mx(ap(o), ap(sc), T.zb[:]), [("zb", A)], [o, sc])

    for sg in range(2):
        w = 16 if sg == 0 else 8
        for h in range(2):
            ts(("dup", S(32 * sg + 16 * h, 32 * sg + 16 * h + w)), ("pI", S(16 * sg, 16 * sg + w)), ("cf", S(h, h + 1)), ALU.mult)
    ts(("p4", S(0, 24)), ("pI", A), 4.0, ALU.mult)
    tr(("dtr", A), ("dup", A))
    tr(("w0", A), ("p4", A))
    for sg in range(2):
        tt(("kof", S(sg, 32, 2)), ("dtr", S(32 * sg, 32 * sg + 16)), ("dtr", S(32 * sg + 16, 32 * sg + 32)), ALU.add)
    for h in range(2):
        cp("a", ("WO", S(2 + 60 * h, 48 + 60 * h, 3)), ("w0", S(16 * h, 16 * h + 16)))
        cp("a", ("Y0", S(5 * h, 5 * h + 4), S(0, 4)), ("w0", S(16 * h, 16 * h + 16)))
    quant("qt0", "st0", 0, 192, "TW0")
    cp("v", ("koff", A), ("kof", A))
    quant("uq", "us", 0, 128, "ub")

    def d1(k, e, lo=0, hi=108):
        name, o = ("D3", 0) if k == 3 else ("WO", 108 * k)
        return (name, S(o + lo, o + hi)) if e is None else (name, S(o + lo + e, o + hi, 3))

    def bulk(t, j):
        if sends_f[t]:
            return
        a, b, far = PIECES[t][j]
        via = relay_of(t, core, to[t], T, topo) if far else None
        qn, sn = ("rq", "rs") if via is not None else ("lq%d" % t, "ls%d" % t)
        sem = ("r%d_%d" if via is not None else "a%d_%d") % (j, t)
        dst = via if via is not None else to[t]
        send(dst, T[qn][:, a:b].bitcast(dt.uint8), T["qt%d" % t][:, a:b].bitcast(dt.uint8), sem, [("qt%d" % t, S(a, b))])
        send(dst, T[sn][:, a:b], T["st%d" % t][:, a:b], sem, [("st%d" % t, S(a, b))])

    def unpack(t, j):
        a, b, far = PIECES[t][j]
        via = relay_of(t, frm[t], core, T, topo) if far else None
        last = via if via is not None else frm[t]
        arrival("a%d_%d" % (j, t), 2 * len(topo.engines(last, core)), [("lq%d" % t, S(a, b)), ("ls%d" % t, S(a, b))])
        for e in range(4):
            mm(4 * (j % 2) + e, "Eq", "Es", 128 * e, "lq%d" % t, "ls%d" % t, a, b)
        for e in range(4):
            cp("a", ("Dt", S(4 * a + e, 4 * b, 4)), bank(4 * (j % 2) + e, b - a))

    def slides(t):
        dst = to[t]
        Lc, Ls = ("L", S(1, 10), S(0, 4)), ("L", S(0, 9), S(1, 5))
        for step in SLIDES:
            kind = step[0]
            k = int(step[1:]) if len(step) > 1 else 2
            K, Z, Y = "K%d" % k, "Z%d" % k, "Y%d" % k
            if kind == "R":
                tt((Z, S(1, 108, 3)), (K,) + right, (K,) + down, ALU.is_ge)
            elif kind == "M":
                tt(("M", A), (K,) + right, (K,) + down, ALU.max)
            elif kind in "abc":
                c = 1 + "abc".index(kind)
                scan(("L", S(1, 10), c), (Z, S(3 * c - 2, 108, 12)), ("L", S(1, 10), c - 1), ALU.max, ALU.min)
            elif kind == "o":
                tt((Z, S(2, 108, 3)), Lc, Ls, ALU.is_gt)
            elif kind == "n":
                tt(("non", A), Lc, Ls, ALU.is_le)
            elif kind == "t":
                tt(("t1", A), (Z, S(2, 108, 3)), ("M", A), ALU.mult)
            elif kind == "u":
                tt(("t2", A), ("non", A), (K,) + cur, ALU.mult)
            elif kind == "K":
                tt((K,) + cur, ("t1", A), ("t2", A), ALU.add)
            elif kind == "A":
                ts((Y,) + cur, d1(k, 2), ("lam", S(k, k + 1)), ALU.min)
            elif kind == "B":
                tt(d1(k, 0), (Y,) + right, (Y,) + down, ALU.subtract)
            elif kind == "C":
                tt(d1(k, 1), (Y,) + down, (Y,) + cur, ALU.subtract)
            elif kind == "W" and k < 3:
                scan(d1(k + 1, None), (Z, A), d1(k, None), ALU.mult, ALU.add)
            elif kind in "WX":
                h = 0 if kind == "W" else 1
                scan(("WF", S(48 * h, 48 * h + 48)), (Z, S(60 * h, 60 * h + 48)), d1(k, None, 60 * h, 60 * h + 48), ALU.mult, ALU.add)
            elif kind == "e":
                scan(("WO", S(324, 387)), (Z, S(0, 63)), d1(k, None, 0, 63), ALU.mult, ALU.add)
            elif kind == "g":
                op("v", lambda: g.vector.tensor_tensor(T.lg[:], T.WO[:, 0:387].indirect(T.lgo[:]), T.tc[:], ALU.add),
                   [("WO", S(0, 387)), ("lgo", A), ("tc", A)], [("lg", A)])
            elif kind == "l":
                tr(("lt", A), ("lg", A))
            else:
                cp("v", ("sl%d" % t, A), ("lt", S(0, 24)))
                if sends_f[t]:
                    gather("a", ("Ft", S(0, 384)), ("TW%d" % t, S(0, 1536)), ("sl%d" % t, A))
                else:
                    send(dst, T["ll%d" % t][:], T["sl%d" % t][:], "al_%d" % t, [("sl%d" % t, A)])
            if sends_f[t] and step == QUANT_F_AFTER:
                quant("fq%d" % t, "fs%d" % t, 0, 128, "Ft")
                send(dst, T["lq%d" % t][:, 0:96].bitcast(dt.uint8), T["fq%d" % t][:, 0:96].bitcast(dt.uint8), "al_%d" % t, [("fq%d" % t, S(0, 96))])
                send(dst, T["ls%d" % t][:, 0:96], T["fs%d" % t][:, 0:96], "al_%d" % t, [("fs%d" % t, S(0, 96))])
        tr(("wt", A), ("WF", S(2, 96, 3)))

    def origins():
        w = ("WF", S(2, 96, 3))
        ts(("o1", A), w, -6.25, ALU.mult, ("cf", S(4, 5)), ALU.add)
        ts(("o2", A), w, float(4 * C), ALU.is_ge)
        ts(("o3", A), w, 0.25, ALU.mult)
        tt(("o4", A), ("o1", A), ("o2", A), ALU.mult)
        tt(("olb", A), ("o3", A), ("o4", A), ALU.add)
        for a in range(4):
            for h in range(2):
                op("s", lambda: g.sync.dma_start(T.ol[2 * a + h:2 * a + h + 1, :], T.olb[32 * a:32 * a + NB, 16 * h:16 * h + 16]),
                   [("olb", A)], [], "sto")

    def keys_to_grids(t):
        gather("a", ("kg", S(256, 512)), ("ks", A), ("koff", S(16, 32)))
        gather("v", ("kg", S(32, 256)), ("ks", A), ("koff", S(2, 16)))
        if t == 0:
            tt(d1(0, 0), ("Y0",) + right, ("Y0",) + down, ALU.subtract)
        tr(("kt", S(32, 256)), ("kg", S(32, 256)))
        tr(("kt", S(256, 512)), ("kg", S(256, 512)))
        if t == 0:
            tt(d1(0, 1), ("Y0",) + down, ("Y0",) + cur, ALU.subtract)
        for h in range(2):
            cp("v", ("K0", S(5 * h, 5 * h + 4), S(0, 4)), ("kt", S(16 * h, 512, 32)))

    def layer(t):
        last = t == ROUNDS - 1
        TW, TN, qn, sn = "TW%d" % t, "TW%d" % (t + 1), "qt%d" % (t + 1), "st%d" % (t + 1)
        for step in LAYER:
            q, kind = step[-1], step[:-1].rstrip("0123")
            d = [int(ch) for ch in step[len(kind):-1]]
            c = d[0]
            a, e = CH[c % 3]
            if kind == "C":
                ts(("voff", S(24 * c, 24 * c + 24)), ("wt", S(0, 24)), float(c), ALU.add)
                if last and c == 1:
                    origins()
                    quant("vq", "vs", 0, 128, "vb")
            elif kind == "F" and gets_f[t]:
                if c == 0:
                    for b in range(4):
                        mm(b, "Eq", "Es", 128 * b, "lq%d" % t, "ls%d" % t, 0, 128)
                if c == 1:
                    for b in range(4):
                        cp("av"[b % 2], (TW, S(1536 + b, 1920, 4)), bank(b, 96))
            elif kind == "F":
                gather(q, (TW, S(1536 + a, 1536 + e)), ("Dt", A), ("ll%d" % t, S(8 * c, 8 * c + 8)))
            elif kind == "G":
                o = 24 * d[1] + 8 * c
                gather(q, ("V", S(4 * a + d[1], 4 * e, 4)), (TW, S(0, 1536 + e)), ("voff", S(o, o + 8)))
            elif kind == "QV":
                quant("qv", "sv", a, e, "V")
                for b in ((0, 2, 3, 1), (0, 1, 2, 3), (1, 2, 3, 0))[c]:
                    mm(4 * (c % 2) + b, "wq", "wsc", 128 * b, "qv", "sv", a, e)
            elif kind == "R":
                o, i = ("rl", S(4 * a + d[1], 4 * e, 4)), bank(4 * (c % 2) + d[1], e - a)
                op("a", lambda: g.scalar.activation(ap(o), ap(i), ACT.Relu, 0.0, 0.015625), [i], [o])
            elif kind == "A":
                w = S(4 * a + d[1], 4 * e, 4)
                tt((TN, w), ("rl", w), ("V", w), ALU.add)
            elif kind == "QT":
                quant(qn, sn, a, e, TN)
                if last:
                    op("s", lambda: g.sync.dma_start(T.oc[:, 4 * a:4 * e], T[qn][:, a:e].bitcast(dt.uint8)), [(qn, S(a, e))], [], "sto")
                else:
                    for j, (pa, pb, far) in enumerate(PIECES[t + 1]):
                        if a < pb <= e:
                            bulk(t + 1, j)
                side = ("vq", "vs") if last else ("uq", "us")
                mm(4 + c, side[0], side[1], 0, qn, sn, a, e)
                if last and c == 2:
                    for k in range(4):
                        op("s", lambda: g.sync.dma_start(T.osc[4 * k:4 * k + 4, :], T[sn][32 * k:32 * k + 4, :]), [(sn, A)], [], "sto")
            else:
                cp(q, ("yb" if last else "ks", S(a, e)), bank(4 + c, e - a))
                if last and c > 0:
                    y0 = 0 if c == 1 else a
                    op("a", lambda: g.scalar.dma_start(T.y[:, y0:e], T.yb[:, y0:e]), [("yb", S(y0, e))], [], "sto")

    bulk(0, 0)
    mm(4, "uq", "us", 0, "qt0", "st0", 0, 192)
    cp("a", ("ks", S(0, 192)), bank(4, 192))
    quant("qt0", "st0", 192, 384, "TW0")
    bulk(0, 1)
    mm(5, "uq", "us", 0, "qt0", "st0", 192, 384)
    cp("a", ("ks", S(192, 384)), bank(5, 192))
    quant("Eq", "Es", 0, 512, "Ef")

    for t in range(ROUNDS):
        keys_to_grids(t)
        if t == 1:
            op("s", lambda: g.sync.dma_start(T.vb[:], T.v[:]), [], [("vb", A)], "dv", after=[len(toks) - 1])
        for j in range(0 if gets_f[t] else len(PIECES[t])):
            unpack(t, j)
        slides(t)
        lanes = len(topo.engines(frm[t], core))
        if gets_f[t]:
            arrival("al_%d" % t, 2 * lanes, [("lq%d" % t, S(0, 96)), ("ls%d" % t, S(0, 96))])
        else:
            arrival("al_%d" % t, lanes, [("ll%d" % t, A)])
        layer(t)

    for sem, val in total.items():
        if known["g"].get(sem, 0) < val:
            g.wait_ge(T.sem[sem], val)
